import numpy as np, ml_dtypes
CORES = [3,11,19,27,35,43,51,59]
N = 8
import mx_ref
BF = ml_dtypes.bfloat16
def entries(a):
    return np.ascontiguousarray(a.T).reshape(-1)
def table(e):
    return np.ascontiguousarray(np.reshape(e, (-1, 16)).T).astype(np.int32)
def cols(t, e):
    v = np.concatenate([t.reshape(128, -1, 4), np.zeros((128, 1, 4), BF)], axis=1)
    return np.ascontiguousarray(v[:, e]).reshape(128, -1)
def cut(t, i, w=512):
    return t[:, w * i:w * i + w]
def f(rng, *shape):
    return mx_ref.flush((rng.standard_normal(shape, dtype=np.float32) * np.exp2(rng.integers(-2, 3, shape[:-1] + (1,)))).astype(BF))
def wide(rng, *shape, cols=0):
    v = rng.standard_normal(shape, dtype=np.float32) * np.exp2(rng.integers(-12, 13, shape)).astype(np.float32)
    if cols: v *= np.repeat(np.exp2(rng.integers(-cols, cols + 1, shape[:-2] + (1, shape[-1] // 4))) * (rng.random(shape[:-2] + (1, shape[-1] // 4)) > 0.0625), 4, axis=-1).astype(np.float32)
    return mx_ref.flush(v.astype(BF))
T, CAPP, F = 128, 96, 8
def inverse(e):
    o = np.full(F * T, -1)
    k = np.flatnonzero(e >= 0); k = k[np.argsort(e[k], kind="stable")]; v = e[k]
    at = np.arange(len(k)) - np.searchsorted(v, v); keep = at < F
    o[(F * v + at)[keep]] = k[keep]
    return o
def counts(rng, most=CAPP):
    n = np.zeros((N, N), int)
    for r in range(N):
        a = rng.integers(T // N, 4 * T // N + 1, N)
        n[:, r] = a + np.bincount(rng.permutation(np.repeat(np.arange(N), most - a))[:4 * T - a.sum()], minlength=N)
    return n
def senders(rng, n):
    return np.stack([rng.permutation(np.repeat(np.arange(N), n[:, r])) for r in range(N)])
def lists(rng, A, node=None, top=None, popular=False, big=None):
    sn = np.full((N, N * CAPP), -1); nb = np.zeros((N, 4 * T), int)
    for s in range(N):
        d, e = np.nonzero(A == s); free = rng.permutation(T)
        if node is not None: v = node[d, e]
        elif top is not None:
            t = top[d, e]; h = (t.sum() + F - 1) // F; v = np.zeros(len(d), int); big.append(free[:h])
            v[t] = rng.permutation(np.repeat(free[:h], F))[:t.sum()]
            v[~t] = rng.permutation(np.repeat(free[h:], F))[:(~t).sum()]
        else:
            h = len(d) // 16 if popular else 0
            v = rng.permutation(np.concatenate([np.repeat(free[:h], F), rng.permutation(np.repeat(free[h:], F))[:len(d) - F * h]]))
        for q in range(N):
            k = np.flatnonzero(d == q); c = rng.permutation(CAPP)[:len(k)]
            sn[s, q * CAPP + c] = v[k]; nb[q, e[k]] = s * CAPP + c
    return {"sn": np.stack([table(a) for a in sn]), "nb": np.stack([table(a) for a in nb]), "il": np.stack([table(inverse(a)) for a in sn])}
def setup_inputs(rng):
    return {"x": f(rng, N, 128, 4 * T), "gr": f(rng, N, 128, 4 * T), "w": np.repeat(f(rng, 1, 128, 2048), N, axis=0), "w2": np.repeat(f(rng, 1, 128, 2048), N, axis=0), **lists(rng, senders(rng, counts(rng)))}
def setup_inputs_ties(rng):
    d = setup_inputs(rng); own = d["x"].reshape(N, 128, T, 4)
    d["x"] = np.ascontiguousarray(np.where(rng.random((N, 1, T, 1)) < 0.7, own[:1], own)).reshape(N, 128, 4 * T)
    n = counts(rng, min(CAPP, T)); A = np.zeros((N, 4 * T), int); node = np.zeros((N, 4 * T), int)
    e = np.arange(4 * T); j = e % T; k = (e // T + j) % 4
    for r in range(N):
        o = rng.permutation(N); to = 4 * rng.permutation(T)[j] + k
        A[r, to] = np.repeat(o, n[o, r]); node[r, to] = rng.permutation(T)[j]
    return {**d, **lists(rng, A, node=node)}
def setup_inputs_oneside(rng):
    d = setup_inputs(rng); top = np.zeros((N, 4 * T), bool); big = []
    for r in range(N): top[r, 4 * rng.permutation(T)[:T // 2] + 3] = True
    d.update(lists(rng, senders(rng, counts(rng)), top=top, big=big))
    v = np.abs(d["x"].astype(np.float32)).reshape(N, 128, T, 4)
    for s in range(N): v[s][:, big[s]] *= 64
    d["x"] = v.reshape(N, 128, 4 * T).astype(BF); d["w"] = np.abs(d["w"].astype(np.float32)).astype(BF)
    return d
def setup_inputs_popular(rng):
    return {**setup_inputs(rng), **lists(rng, senders(rng, counts(rng)), popular=True)}
def setup_inputs_full(rng):
    n = np.zeros((N, N), int); o = rng.permutation(N); at = rng.permutation(N)
    m = 4 * T // CAPP; rest = 4 * T - m * CAPP
    for r in range(N):
        for j in range(m): n[o[(at[r] + j) % N], r] = CAPP
        if rest: n[o[(at[r] + m) % N], r] = rest
    return {**setup_inputs(rng), **lists(rng, senders(rng, n))}
def setup_inputs_spread(rng):
    d = setup_inputs(rng); d["x"] = wide(rng, N, 128, 4 * T, cols=8); return d
def check_inputs(d):
    b = []
    for t in ("w", "w2"):
        if (d[t] != d[t][:1]).any(): b.append(t)
    e = np.stack([entries(a) for a in d["sn"]])
    if e.min() < -1 or e.max() >= T: b.append("sn")
    e = np.clip(e, -1, T - 1)
    for r in range(N):
        if np.bincount(e[r][e[r] >= 0], minlength=T).max() > F: b.append("sn")
        if not np.array_equal(np.sort(entries(d["nb"][r])), np.flatnonzero(e[:, r * CAPP:(r + 1) * CAPP].reshape(-1) >= 0)): b.append("nb")
        if not np.array_equal(entries(d["il"][r]), inverse(e[r])): b.append("il")
    return b
def four(v):
    return [mx_ref.quantize(np.ascontiguousarray(cut(v, b))) for b in range(4)]
def reference(x, gr, w, w2, sn, nb, il):
    G = []
    for r in range(N):
        arrived = mx_ref.quantize(np.concatenate([cols(x[s], entries(sn[s])[r * CAPP:(r + 1) * CAPP]) for s in range(N)], axis=1))
        e = entries(nb[r])
        z = [mx_ref.matmul(W, arrived)[:, e].reshape(128, T, 4) + np.float32(0.0) for W in four(w[r])]
        win = np.stack([v.argmax(axis=2) for v in z], axis=2)
        g = gr[r].reshape(128, T, 4); back = np.zeros((128, N * CAPP, 4), BF)
        for k in range(4): back[:, e[k::4]] = np.where(win == k, g, np.zeros_like(g))
        G.append(back)
    y = np.zeros((N, 128, 4 * T), np.float32)
    for s in range(N):
        q = mx_ref.quantize(np.concatenate([G[r][:, s * CAPP:(s + 1) * CAPP].reshape(128, -1) for r in range(N)], axis=1))
        e = entries(il[s])
        for b, V in enumerate(four(w2[s])):
            u = mx_ref.matmul(V, q); t = np.zeros((128, T), np.float32)
            for i in range(F):
                k = e[i::F]; has = k >= 0
                t[:, has] += u[:, k[has]]
            y[s][:, T * b:T * b + T] = t
    return {"y": y}

import numpy as np
from concourse.bass import DstId, RemoteDMATransfer
from concourse.mybir import dt, AluOpType, ActivationFunctionType

N, NT, CAP, HB = 8, 128, 96, 384
UW = 776
CODES = "float8_e4m3fn_x4"

SCRATCH = {
    "xb": ("sbuf", [128, 528], "bfloat16"),
    "snw": ("sbuf", [128, 48], "int32"),
    "snof": ("sbuf", [128, 192], "uint16"),
    "xt": ("sbuf", [128, 3072], "bfloat16"),
    "fc": ("sbuf", [128, 768], CODES), "fs": ("sbuf", [128, 768], "uint8"),
    "rc": ("sbuf", [128, 768], CODES), "rs": ("sbuf", [128, 768], "uint8"),
    "wb": ("sbuf", [128, 2048], "bfloat16"),
    "wq": ("sbuf", [128, 512], CODES), "ws": ("sbuf", [128, 512], "uint8"),
    "vb": ("sbuf", [128, 2048], "bfloat16"),
    "vq": ("sbuf", [128, 512], CODES), "vs": ("sbuf", [128, 512], "uint8"),
    "zp": ("psum", [128, 4096], "float32"),
    "zb": ("sbuf", [128, 3072], "float32"),
    "nbd": ("dram", [16, 32], "int32"),
    "nbw": ("sbuf", [128, 32], "int32"),
    "zof": ("sbuf", [128, 64], "uint16"),
    "pa": ("sbuf", [128, 32], "int32"), "pb": ("sbuf", [128, 32], "int32"),
    "pc": ("sbuf", [128, 32], "int32"), "pd": ("sbuf", [128, 32], "int32"),
    "pof": ("sbuf", [128, 32], "uint16"),
    "ivv": ("sbuf", [128, 512], "int32"),
    "inv": ("sbuf", [128, 768], "int32"),
    "invw": ("sbuf", [128, 48], "int32"),
    "ivo": ("sbuf", [128, 48], "uint16"),
    "pi": ("sbuf", [128, 1], "int32"),
    "k15": ("sbuf", [128, 1], "int32"), "k3": ("sbuf", [128, 1], "int32"), "k12": ("sbuf", [128, 1], "int32"),
    "f8": ("sbuf", [128, 1], "float32"), "f12": ("sbuf", [128, 1], "float32"), "fgr": ("sbuf", [128, 1], "float32"),
    "ilpat": ("sbuf", [128, 64], "int32"), "grpat": ("sbuf", [128, 32], "int32"),
    "grb": ("sbuf", [128, 512], "bfloat16"), "gro": ("sbuf", [128, 32], "uint16"),
    "z0": ("sbuf", [128, 512], "float32"), "m1": ("sbuf", [128, 512], "float32"), "m2": ("sbuf", [128, 512], "float32"),
    "d0": ("sbuf", [128, 2048], "bfloat16"), "d1": ("sbuf", [128, 2048], "bfloat16"),
    "rr": ("sbuf", [128, 4096], "bfloat16"), "e0": ("sbuf", [128, 4096], "bfloat16"),
    "gg": ("sbuf", [128, 4096], "bfloat16"),
    "h": ("sbuf", [128, 3072], "bfloat16"),
    "bc": ("sbuf", [128, 768], CODES), "bs": ("sbuf", [128, 768], "uint8"),
    "qc": ("sbuf", [128, 768], CODES), "qs": ("sbuf", [128, 768], "uint8"),
    "ub": ("sbuf", [128, 4 * UW], "float32"),
    "ilf": ("sbuf", [128, 1024], "int32"), "ilo": ("sbuf", [128, 64], "uint16"),
    "ilp": ("sbuf", [128, 1024], "int32"), "ilw": ("sbuf", [128, 64], "int32"),
    "ila": ("sbuf", [128, 64], "int32"), "ilb": ("sbuf", [128, 64], "int32"),
    "ilq": ("sbuf", [128, 64], "uint16"),
    "a0": ("sbuf", [128, 1024], "float32"), "a1": ("sbuf", [128, 1024], "float32"),
    "a2": ("sbuf", [128, 1024], "float32"), "a3": ("sbuf", [128, 1024], "float32"),
    "yb": ("sbuf", [128, 512], "float32"),
}
SEMAPHORES = ["cv", "cs", "ct", "cp", "d_x", "d_sn", "d_w", "d_v", "d_gr", "d_nd", "d_nb", "d_il", "d_iv", "d_ih",
              "d_of", "d_ob", "d_y", "fa0", "fa1", "ba0", "ba1", "ls"]


def half_sends(s, half, cores, topo):
    ds = [d for d in range(4 * half, 4 * half + 4) if d != s]
    if len(ds) == 4:
        cut_c = cut_p = [(0, 2), (2, 4), (4, 6), (6, 8)]
    else:
        cut_c, cut_p = [(0, 4), (4, 6), (6, 8)], [(0, 2), (2, 4), (4, 8)]
    out = []
    for d, (a, b), (u, v) in zip(ds, cut_c, cut_p):
        e = topo.engines(cores[s], cores[d])
        out.append((d, e[a:b], e[u:v]))
    return out


def arrivals(r, half, cores, topo):
    n = 0
    for s in range(4 * half, 4 * half + 4):
        if s != r:
            for d, ec, ep in half_sends(s, r // 4, cores, topo):
                if d == r:
                    n += len(ec) + len(ep)
    return n


def rank_program(g, core, T, topo):
    r = T.rank_of(core)
    if r is None:
        return
    A, COPY, IDENT = AluOpType, ActivationFunctionType.Copy, ActivationFunctionType.Identity
    cores = list(T.cores)
    hr, ho = r // 4, 1 - r // 4
    V, S, P, Y = g.vector, g.scalar, g.tensor, g.sync
    qn = {"V": V, "S": S, "P": P, "Y": Y, "G": g}
    cnt, seen = {}, {}

    def done(ins, sem, n=1):
        ins.then_inc(T.sem[sem], n)
        cnt[sem] = cnt.get(sem, 0) + n
        return (sem, cnt[sem])

    def need(q, *marks):
        best = {}
        for m in marks:
            if m is not None:
                best[m[0]] = max(best.get(m[0], 0), m[1])
        for sem, val in best.items():
            if seen.get((q, sem), 0) < val:
                qn[q].wait_ge(T.sem[sem], val)
                seen[(q, sem)] = val

    def dv(ins): return done(ins, "cv")
    def ds(ins): return done(ins, "cs")
    def dp(ins): return done(ins, "ct")
    def dg(ins): return done(ins, "cp")

    x_in = done(S.dma_start(T.xb[:, 16:528], T.x[:, :]), "d_x", 16)
    for k in range(5):
        done(Y.dma_start(T.snw[16 * k:16 * k + 16, :], T.sn[:, :]), "d_sn", 16)
    for k in range(5, 8):
        sn_in = done(S.dma_start(T.snw[16 * k:16 * k + 16, :], T.sn[:, :]), "d_sn", 16)
    for k in range(4):
        nd_in = done(Y.dma_start(T.nbd[:, 8 * k:8 * k + 8], T.nb[k:16:4, :]), "d_nd", 16)
    w_in = done(Y.dma_start(T.wb[:, :], T.w[:, :]), "d_w", 16)
    gr_in = done(S.dma_start(T.grb[:, :], T.gr[:, :]), "d_gr", 16)
    need("Y", nd_in)
    for k in range(8):
        nb_in = done(Y.dma_start(T.nbw[16 * k:16 * k + 16, :], T.nbd[:, :]), "d_nb", 16)
    v_in = done(Y.dma_start(T.vb[:, :], T.w2[:, :]), "d_v", 16)

    m_pi = dg(g.iota(T.pi[:, :], [[0, 1]], 0, 1))
    m_grp = dg(g.iota(T.grpat[:, :], [[1, 4], [16, 8]], 0, 0))
    m_ivv = dg(g.iota(T.ivv[:, :], [[-2, 4], [8, 128]], 7, 0))
    m_ilp = dg(g.iota(T.ilpat[:, :], [[1, 8], [512, 2], [128, 4]], 0, 0))

    m_pad = dv(V.memset(T.xb[:, 0:16], 0.0))
    need("V", m_pi)
    k15 = dv(V.tensor_scalar(T.k15[:, :], T.pi[:, :], 15, None, A.bitwise_and))
    k3 = dv(V.tensor_scalar(T.k3[:, :], T.pi[:, :], 3, None, A.bitwise_and))
    k12 = dv(V.tensor_scalar(T.k12[:, :], T.pi[:, :], 12, None, A.bitwise_and))
    m_ilf = dv(V.memset(T.ilf[:, :], 0))
    m_inv = dv(V.memset(T.inv[:, :], 0))
    need("V", k12)
    m_f8 = dv(V.tensor_scalar(T.f8[:, :], T.k15[:, :], 8, None, A.mult))
    m_f12 = dv(V.tensor_copy(T.f12[:, :], T.k12[:, :]))
    need("Y", m_ilf)
    il_in = done(Y.dma_start(T.ilf[0:1, :], T.il[:, :]), "d_il", 16)

    need("V", sn_in)
    snof = []
    for t in range(4):
        snof.append(dv(V.tensor_scalar(T.snof[:, 48 * t:48 * t + 48], T.snw[:, :], 4, 16 + t, A.mult, A.add)))

    def sends(codes, planes, lc, lp, half, sem):
        for own, land, w in ((codes, lc, 0), (planes, lp, 1)):
            tr = []
            for d, ec, ep in half_sends(r, half, cores, topo):
                rid, pid, _ = topo.addr(cores[d])
                mask = sum(1 << e for e in (ep if w else ec))
                src, dst = own[:, CAP * d:CAP * d + CAP], land[:, CAP * r:CAP * r + CAP]
                if not w:
                    src, dst = src.bitcast(dt.uint8), dst.bitcast(dt.uint8)
                tr.append(RemoteDMATransfer(dst_ids=[DstId(rid=rid, pnc=pid)], dma_engine_mask=mask,
                                            remote_sem=T.sem[sem], srcs=[src], dsts=[dst]))
                cnt["ls"] = cnt.get("ls", 0) + len(ep if w else ec)
            g.remote_dma_fused(tr, local_sem=T.sem["ls"])

    def own_block(codes, planes, lc, lp, sem):
        a, b = CAP * r, CAP * r + CAP
        done(Y.dma_start(lc[:, a:b].bitcast(dt.uint8), codes[:, a:b].bitcast(dt.uint8)), sem, 16)
        return done(Y.dma_start(lp[:, a:b], planes[:, a:b]), sem, 16)

    for half in (ho, hr):
        win = T.xb[:, 0:528]
        marks = []
        for q, t in (("S", 0), ("V", 2), ("S", 1), ("V", 3)):
            need(q, x_in, m_pad, snof[t])
            out = T.xt[:, 4 * HB * half + t:4 * HB * (half + 1):4]
            src = win.indirect(T.snof[:, 48 * t + 24 * half:48 * t + 24 * half + 24])
            marks.append(ds(S.activation(out, src, COPY)) if q == "S" else dv(V.tensor_copy(out, src)))
        need("V", *marks)
        f_q = dv(V.quantize_mx(T.fc[:, HB * half:HB * half + HB], T.fs[:, HB * half:HB * half + HB],
                               T.xt[:, 4 * HB * half:4 * HB * half + 4 * HB]))
        need("G", f_q)
        sends(T.fc, T.fs, T.rc, T.rs, half, "fa%d" % hr)
    need("Y", f_q)
    own_f = own_block(T.fc, T.fs, T.rc, T.rs, "d_of")

    m_rr = dg(g.iota(T.rr[:, 1:4096:2], [[0, 2048]], 0, 0, allow_small_or_imprecise_dtypes=True))
    m_ee = dg(g.iota(T.e0[:, 0:4096:2], [[0, 2048]], 0, 0, allow_small_or_imprecise_dtypes=True))
    m_e1 = dg(g.iota(T.e0[:, 7:4096:8], [[0, 512]], 1, 0, allow_small_or_imprecise_dtypes=True))

    m_d1 = dv(V.memset(T.d1[:, :], 0.0))
    need("V", m_f12, k3)
    m_fgr = dv(V.tensor_scalar(T.fgr[:, :], T.k3[:, :], 128, T.f12[:, :], A.mult, A.add))
    need("V", w_in)
    w_q = dv(V.quantize_mx(T.wq[:, 0:512], T.ws[:, 0:512], T.wb[:, 0:2048]))
    need("V", m_fgr, m_grp)
    m_gro = dv(V.tensor_scalar(T.gro[:, :], T.grpat[:, :], T.fgr[:, :], None, A.add))
    need("S", m_d1, m_gro, gr_in)
    d1_ok = ds(S.activation(T.d1[:, 0:2048:4], T.grb[:, 0:512].indirect(T.gro[:, 0:32]), COPY))

    need("V", nb_in)
    p_a = dv(V.tensor_scalar(T.pa[:, :], T.nbw[:, :], 15, None, A.bitwise_and))
    p_b = dv(V.tensor_scalar(T.pb[:, :], T.nbw[:, :], 4, None, A.arith_shift_right))
    need("V", p_a)
    p_c = dv(V.tensor_scalar(T.pc[:, :], T.pa[:, :], 48, None, A.mult))
    m_zo = None
    for k in range(4):
        for bl in range(2):
            m_zo = dv(V.tensor_scalar(T.zof[:, 16 * k + 8 * bl:16 * k + 8 * bl + 8], T.nbw[:, 8 * k:8 * k + 8],
                                      768 * bl, None, A.add))
            if (k, bl) == (0, 1):
                need("V", p_c)
                p_d = dv(V.tensor_tensor(T.pd[:, :], T.pc[:, :], T.pb[:, :], A.add))
    need("V", p_d)
    p_of = dv(V.tensor_copy(T.pof[:, :], T.pd[:, :]))
    m_d0 = dv(V.memset(T.d0[:, 0:2048:4], 0.0))
    need("V", p_of, m_inv, m_ivv)
    m_sc = dv(V.tensor_copy(T.inv[:, 0:768].indirect(T.pof[:, 0:32]), T.ivv[:, :]))
    need("Y", m_sc)
    for k in range(8):
        iv_in = done(Y.dma_start(T.invw[16 * k:16 * k + 16, :], T.inv[0:1, :]), "d_iv", 16)
    for b in range(4):
        m_up = dv(V.memset(T.ub[:, UW * b + 768:UW * b + UW], 0.0))
    need("V", m_f8, m_ilp)
    m_ilo = dv(V.tensor_scalar(T.ilo[:, :], T.ilpat[:, :], T.f8[:, :], None, A.add))

    zp_free = {}

    def products(half, codes, planes, st, sts, ready, who, land, wide):
        need("P", *ready)
        mm = []
        for b in range(4):
            at = 512 * (2 * b + half)
            need("P", zp_free.get((b, half)))
            mm.append(dp(P.matmul_mx(T.zp[:, at:at + HB], st[:, 128 * b:128 * b + 128], sts[:, 128 * b:128 * b + 128],
                                     codes[:, HB * half:HB * half + HB], planes[:, HB * half:HB * half + HB], True, True)))

        def take(b):
            at = 512 * (2 * b + half)
            need(who[b], mm[b])
            out, src = land[:, wide * b + HB * half:wide * b + HB * half + HB], T.zp[:, at:at + HB]
            m = ds(S.activation(out, src, COPY)) if who[b] == "S" else dv(V.tensor_copy(out, src))
            zp_free[(b, half)] = m
            return m
        return take

    zb_ok = {}
    fa = {h: ("fa%d" % h, arrivals(r, h, cores, topo)) for h in (0, 1)}
    take = products(ho, T.rc, T.rs, T.wq, T.ws, (w_q, fa[ho]), "SVSV", T.zb, 768)
    for b in range(4):
        zb_ok[(b, 0)] = take(b)
    take = products(hr, T.rc, T.rs, T.wq, T.ws, (fa[hr], own_f), "SVVS", T.zb, 768)
    for b in (0, 1, 2):
        zb_ok[(b, 1)] = take(b)

    def zpick(p, k):
        return T.zb[:, 1536 * p:1536 * p + 1536].indirect(T.zof[:, 16 * k:16 * k + 16])

    def seg(name, p):
        return T[name][:, 256 * p:256 * p + 256]

    z0_ok, c = {}, {}
    for p in (0, 1):
        if p:
            zb_ok[(3, 1)] = take(3)
        zready = [zb_ok[(b, i)] for b in (2 * p, 2 * p + 1) for i in (0, 1)]
        need("S", m_zo, *zready)
        c["z", p] = zready
        z0_ok[p] = ds(S.activation(seg("z0", p), zpick(p, 0), COPY))

    def nrec(p, k):
        return T.d0[:, 1024 * p + 4 - k:1024 * p + 1024:4]

    def vmax(p, k):
        src, dst = (("z0", "m1"), ("m1", "m2"))[k - 1]
        need("V", m_zo, z0_ok[p] if k == 1 else c["m1", p], *c["z", p])
        c[dst, p] = dv(V.tensor_tensor(seg(dst, p), zpick(p, k), seg(src, p), A.max))

    def vrec(p, k):
        src = ("z0", "m1", "m2")[k - 1]
        need("V", m_zo, m_d0, z0_ok[p] if k == 1 else c[src, p], *c["z", p])
        c["n", p, k] = dv(V.tensor_tensor(nrec(p, k), zpick(p, k), seg(src, p), A.is_le))

    def srec(p, k):
        need("S", c["n", p, k], m_e1)
        o = 2048 * p + 7 - 2 * k
        c["r", p, k] = ds(S.activation(T.e0[:, o:2048 * p + 2048:8], nrec(p, k), IDENT, bias=1.0, scale=-1.0))

    def scan1(p):
        need("V", m_d0, d1_ok, m_rr, *[c["n", p, k] for k in (1, 2, 3)])
        c["s1", p] = dv(V.tensor_tensor_scan(T.rr[:, 2048 * p:2048 * p + 2048:2], T.d0[:, 1024 * p:1024 * p + 1024],
                                             T.d1[:, 1024 * p:1024 * p + 1024], 0.0, A.mult, A.add))

    def scan2(p):
        need("V", m_rr, m_ee, m_e1, c["s1", p], *[c["r", p, k] for k in (1, 2, 3)])
        c["s2", p] = dv(V.tensor_tensor_scan(T.gg[:, 2048 * p:2048 * p + 2048], T.e0[:, 2048 * p:2048 * p + 2048],
                                             T.rr[:, 2048 * p:2048 * p + 2048], 0.0, A.mult, A.add))

    h_ok = {}

    def place(q, b, lo, hi):
        need(q, iv_ok[0], c["s2", b // 2])
        out = T.h[:, 4 * lo + b:4 * hi:4]
        src = T.gg[:, 1024 * b:1024 * b + 1024].indirect(T.ivo[:, lo // 16:hi // 16])
        h_ok[(q, b, lo)] = ds(S.activation(out, src, COPY)) if q == "S" else dv(V.tensor_copy(out, src))

    vmax(0, 1); vrec(0, 1); srec(0, 1)
    vmax(0, 2); vrec(0, 2); srec(0, 2)
    vrec(0, 3); srec(0, 3)
    vmax(1, 1); scan1(0); vrec(1, 1); scan2(0)
    need("V", iv_in)
    iv_ok = [dv(V.tensor_copy(T.ivo[:, :], T.invw[:, :]))]
    place("S", 0, 0, 768)
    vmax(1, 2); srec(1, 1); vrec(1, 2); vrec(1, 3); srec(1, 2); srec(1, 3)
    place("S", 1, 0, 768)
    scan1(1); scan2(1)
    for half in (ho, hr):
        place("S", 2, HB * half, HB * half + HB)
        place("V", 3, HB * half, HB * half + HB)
        need("V", *h_ok.values())
        b_q = dv(V.quantize_mx(T.bc[:, HB * half:HB * half + HB], T.bs[:, HB * half:HB * half + HB],
                               T.h[:, 4 * HB * half:4 * HB * half + 4 * HB]))
        need("G", b_q)
        sends(T.bc, T.bs, T.qc, T.qs, half, "ba%d" % hr)
    need("Y", b_q)
    own_b = own_block(T.bc, T.bs, T.qc, T.qs, "d_ob")

    need("V", m_ilo, il_in, m_ilf)
    m_ip = dv(V.tensor_copy(T.ilp[:, :], T.ilf[:, 0:1024].indirect(T.ilo[:, 0:64])))
    need("Y", m_ip)
    for k in range(8):
        ih_in = done(Y.dma_start(T.ilw[16 * k:16 * k + 16, :], T.ilp[0:1, :]), "d_ih", 16)
    need("V", v_in)
    v_q = dv(V.quantize_mx(T.vq[:, 0:512], T.vs[:, 0:512], T.vb[:, 0:2048]))
    need("V", ih_in)
    m_a = dv(V.tensor_scalar(T.ila[:, :], T.ilw[:, :], 0, 769, A.is_lt, A.mult))
    need("V", m_a)
    m_b = dv(V.tensor_tensor(T.ilb[:, :], T.ilw[:, :], T.ila[:, :], A.add))
    need("V", m_b)
    m_iq = dv(V.tensor_copy(T.ilq[:, :], T.ilb[:, :]))

    ba = {h: ("ba%d" % h, arrivals(r, h, cores, topo)) for h in (0, 1)}
    ub_ok = {}
    take = products(ho, T.qc, T.qs, T.vq, T.vs, (v_q, ba[ho]), "SVSV", T.ub, UW)
    for b in range(4):
        ub_ok[(b, 0)] = take(b)
    take = products(hr, T.qc, T.qs, T.vq, T.vs, (ba[hr], own_b), "SVSS", T.ub, UW)

    def upick(b, s):
        return T.ub[:, UW * b:UW * b + UW].indirect(T.ilq[:, 16 * s:16 * s + 16])

    def blk(name, b):
        return T[name][:, 256 * b:256 * b + 256]

    acc = {}

    def first(b):
        need("S", m_iq, m_up, ub_ok[(b, 0)], ub_ok[(b, 1)])
        acc[b] = ds(S.activation(blk("a0", b), upick(b, 0), COPY))

    ub_ok[(0, 1)] = take(0); ub_ok[(1, 1)] = take(1)
    first(0); first(1)
    for b in (2, 3):
        ub_ok[(b, 1)] = take(b)
        first(b)
    for p in (0, 1):
        for s in (1, 2, 3):
            for b in (2 * p, 2 * p + 1):
                need("V", m_iq, m_up, acc[b], ub_ok[(b, 0)], ub_ok[(b, 1)])
                acc[b] = dv(V.tensor_tensor(blk("a%d" % s, b), upick(b, s), blk("a%d" % (s - 1), b), A.add))
        for b in (2 * p, 2 * p + 1):
            need("V", acc[b])
            y_ok = dv(V.tensor_tensor(T.yb[:, 128 * b:128 * b + 128], T.a3[:, 256 * b:256 * b + 128],
                                      T.a3[:, 256 * b + 128:256 * b + 256], A.add))
        need("Y", y_ok)
        y_out = done(Y.dma_start(T.y[:, 256 * p:256 * p + 256], T.yb[:, 256 * p:256 * p + 256]), "d_y", 16)
    need("Y", y_out)
    need("G", ("ls", cnt["ls"]))
